import numpy as np
import ml_dtypes


def mxq(x, axis, fmt="e4m3"):
    dtype, down = {"e4m3": (ml_dtypes.float8_e4m3fn, 7), "e5m2": (ml_dtypes.float8_e5m2, 14)}[fmt]
    v = np.moveaxis(np.asarray(x, np.float32).astype(ml_dtypes.bfloat16).astype(np.float64), axis, -1)
    blocks = v.reshape(v.shape[:-1] + (-1, 32))
    amax = np.abs(blocks).max(-1, keepdims=True)
    byte = np.maximum(np.where(amax > 0, np.frexp(amax)[1] - 1 + 127, 0) - down, 1)
    scale = np.exp2(byte - 127.0)
    codes = (blocks / scale).astype(np.float32).astype(dtype).astype(np.float64)
    return np.moveaxis((codes * scale).reshape(v.shape), -1, axis)


WIDE = False


def mx_kscale(k):
    if not WIDE:
        return np.ones(k)
    levels = np.array([10, -10, 5, -5, 0])
    if k % 512:
        return np.exp2(np.random.permutation(np.resize(levels, k // 32))).repeat(32)
    a = np.empty((k // 512, 16))
    for p in range(k // 512):
        a[p, :8] = np.random.permutation(np.resize(levels, 8))
        for g in range(8):
            far = levels[np.abs(levels - a[p, g]) >= 10]
            a[p, g + 8] = far[np.random.randint(len(far))]
    return np.exp2(a.ravel()).repeat(32)


def f64(x):
    return np.asarray(x).astype(np.float64)


def striped(idx):
    return np.tile(idx.reshape(-1, 16).T, (8, 1)).astype(np.uint16)


def unstriped(offs):
    return offs[:16].T.reshape(-1).astype(np.int64)


E2M1 = np.array([0.0, 0.5, 1.0, 1.5, 2.0, 3.0, 4.0, 6.0, -0.0, -0.5, -1.0, -1.5, -2.0, -3.0, -4.0, -6.0])


def pack_weight(w, fmt):
    k, n = w.shape
    w = f64(np.asarray(w, np.float32).astype(ml_dtypes.bfloat16)).reshape(k // 32, 32, n)
    amax = np.abs(w).max(1)
    if fmt == "e4m3":
        byte = np.frexp(amax)[1] - 1 + 127 - 7
    else:
        mant, ex = np.frexp(amax / 6.0)
        byte = np.where(mant > 0.5, ex, ex - 1) + 127
    byte = np.clip(np.where(amax > 0, byte, 1), 1, 254)
    scaled = (w * np.exp2(127.0 - byte)[:, None, :]).reshape(k, n).astype(np.float32)
    by_word = np.ascontiguousarray(scaled.reshape(k // 512, 128, 4, n).transpose(0, 1, 3, 2))
    if fmt == "e4m3":
        words = by_word.astype(ml_dtypes.float8_e4m3fn).view(np.uint8)
    else:
        c = by_word.astype(ml_dtypes.float4_e2m1fn).view(np.uint8) & 0xF
        words = (c[..., 0::2] | (c[..., 1::2] << 4)).reshape(k // 512, 128, 2 * n)
    return np.ascontiguousarray(words), np.ascontiguousarray(byte.astype(np.uint8).reshape(k // 512, 16, n))


def unpack_weight(words, scales, fmt):
    g, _, n = scales.shape
    words = np.ascontiguousarray(words).reshape(g, 128, n, -1)
    if fmt == "e4m3":
        vals = words.view(ml_dtypes.float8_e4m3fn).astype(np.float64)
    else:
        nib = np.empty((g, 128, n, 4), np.uint8)
        nib[..., 0::2] = words & 0xF
        nib[..., 1::2] = words >> 4
        vals = E2M1[nib]
    vals = vals * np.repeat(np.exp2(scales.astype(np.float64) - 127.0), 8, axis=1)[..., None]
    return vals.transpose(0, 1, 3, 2).reshape(g * 512, n)


def gelu(v):
    return 0.5 * v * (1.0 + np.tanh(np.sqrt(2.0 / np.pi) * (v + 0.044715 * v**3)))


def bf(x):
    return np.asarray(x, np.float32).astype(ml_dtypes.bfloat16)


def planes(Y):
    n, m = Y.shape
    b = f64(bf(Y)).reshape(n // 32, 32, m)
    amax = np.abs(b).max(1)
    byte = np.clip(np.where(amax > 0, np.frexp(amax)[1] - 1 + 127 - 7, 1), 1, 254)
    codes = (b * np.exp2(127.0 - byte)[:, None, :]).reshape(n, m).astype(np.float32).astype(ml_dtypes.float8_e4m3fn).view(np.uint8)
    words = codes.reshape(n // 512, 128, 4, m).transpose(0, 1, 3, 2)
    return np.ascontiguousarray(words), np.ascontiguousarray(byte.astype(np.uint8).reshape(n // 512, 16, m))


K, H, T, S, P1, P2, P3, N = 1024, 512, 4096, 2048, 1024, 512, 256, 1024

def setup_inputs():
    n = np.random.standard_normal
    s = mx_kscale(K)[:, None]
    u = mx_kscale(H)[:, None]
    tab_words, tab_scales = pack_weight(n((K, T)) * s, "e4m3")
    w2_words, w2_scales = pack_weight(0.54 * n((K, H)) / np.sqrt(K) / s, "e2m1")
    spread = np.exp(0.8 * n(N))[None, :]
    return {
        "tab_words": tab_words, "tab_scales": tab_scales,
        "offs": striped(np.random.permutation(T)[:S]),
        "w1": (1.2 * n((K, H)) / np.sqrt(K) / s).astype(np.float32),
        "w2_words": w2_words, "w2_scales": w2_scales,
        "pos1": striped(np.random.permutation(S)[:P1]),
        "pos2": striped(np.random.permutation(S)[:P1]),
        "pos3": striped(np.random.permutation(P1)[:P2]),
        "pos4": striped(np.random.permutation(P1)[:P2]),
        "pos5": striped(np.random.permutation(P2)[:P3]),
        "pos6": striped(np.random.permutation(P2)[:P3]),
        "gain": (np.exp(0.3 * n(H)) * u[:, 0]).astype(np.float32),
        "w3": (n((H, N)) / np.sqrt(H) * spread / u).astype(np.float32),
    }

def reference(tab_words, tab_scales, offs, w1, w2_words, w2_scales, pos1, pos2, pos3, pos4, pos5, pos6, gain, w3):
    v = unpack_weight(tab_words, tab_scales, "e4m3")[:, unstriped(offs)]
    w2 = unpack_weight(w2_words, w2_scales, "e2m1")
    style = mxq(f64(w1), 0, "e4m3").T @ v
    phase = w2.T @ v
    h = np.tanh(style) + np.sin(phase)
    a1 = np.maximum(h[:, unstriped(pos1)], h[:, unstriped(pos2)])
    a2 = f64(gain)[:, None] * a1[:, unstriped(pos3)] * a1[:, unstriped(pos4)]
    a3 = a2[:, unstriped(pos5)] + a2[:, unstriped(pos6)]
    y = mxq(f64(w3), 0, "e4m3").T @ mxq(a3, 0, "e4m3")
    words, scales = planes(y)
    return y, words, scales

@@ -1,0 +1,276 @@
+import math
+from contextlib import ExitStack
+
+import concourse.mybir as mybir
+from concourse.masks import make_identity
+
+K, H, T, S, P1, P2, P3, N = 1024, 512, 4096, 2048, 1024, 512, 256, 1024
+FLOPS = 2 * (2 * K * H * S + H * N * P3)
+
+F32 = mybir.dt.float32
+BF16 = mybir.dt.bfloat16
+I32 = mybir.dt.int32
+U32 = mybir.dt.uint32
+U16 = mybir.dt.uint16
+U8 = mybir.dt.uint8
+E4M3 = mybir.dt.float8_e4m3fn_x4
+E2M1 = mybir.dt.float4_e2m1fn_x4
+ALU = mybir.AluOpType
+ACT = mybir.ActivationFunctionType
+
+P = 128
+PACK = 4
+PASSES = K // (P * PACK)
+CHUNK = 512
+CHUNKS = S // CHUNK
+BLOCKS = CHUNK // P
+TURN = 2.0 * math.pi
+BIG = 1.5 * 2.0**23
+BIG_BITS = float(0x4B400000)
+STEP = 128.0
+SPARE = 32 - 4 * PASSES
+
+
+def tile_list_olympiad_paper_features_kernel(
+    tc, tab_words, tab_scales, offs, w1, w2_words, w2_scales, pos1, pos2, pos3, pos4, pos5, pos6, gain, w3, out_0, out_1, out_2
+):
+    nc = tc.nc
+    with ExitStack() as ctx:
+        lists = ctx.enter_context(tc.tile_pool(name="lists", bufs=1))
+        keep = ctx.enter_context(tc.tile_pool(name="keep", bufs=1))
+        work = ctx.enter_context(tc.tile_pool(name="work", bufs=2))
+        psum = ctx.enter_context(tc.psum_pool(name="psum", bufs=1))
+
+        def load_list(src, name):
+            tile = lists.tile(list(src.shape), U16, name=name)
+            nc.sync.dma_start(tile[:], src)
+            return tile
+
+        table_scales = keep.tile([P, T], U8, name="table_scales", tag="w1_raw0", align_bytes=64)
+        w2_raw_scales = keep.tile([P, PASSES * H], U8, name="w2_raw_scales", align_bytes=64)
+        nc.gpsimd.memset(w2_raw_scales[:].bitcast(I32), 0)
+        for q in range(4):
+            engine = nc.vector if q % 2 == 0 else nc.gpsimd
+            engine.memset(table_scales[32 * q : 32 * q + SPARE, :].bitcast(I32), 0)
+        v_scales = [keep.tile([P, S], U8, name=f"v_scales{a}", align_bytes=64) for a in range(PASSES)]
+        for a in range(PASSES):
+            nc.gpsimd.memset(v_scales[a][:].bitcast(I32), 0)
+        identity = keep.tile([P, P], F32, name="identity")
+        make_identity(nc, identity[:])
+        minus_big = keep.tile([P, P], F32, name="minus_big")
+        nc.gpsimd.memset(minus_big[:], -BIG)
+
+        idx = load_list(offs, "idx")
+        for q in range(4):
+            nc.sync.dma_start(
+                table_scales[32 * q + SPARE : 32 * (q + 1), :].bitcast(I32),
+                tab_scales[:, 4 * q : 4 * q + 4, :].bitcast(I32),
+            )
+        table_words = [keep.tile([P, T], I32, name=f"table_words{a}", tag=f"table{a}", align_bytes=64) for a in range(PASSES)]
+
+        def load_table(a):
+            nc.sync.dma_start(table_words[a][:], tab_words[a].rearrange("p t i -> p (t i)").bitcast(I32))
+
+        def load_w1(a):
+            raw = keep.tile([P, PACK, H], F32, name=f"w1_raw{a}", tag=f"w1_raw{a}", align_bytes=64)
+            nc.sync.dma_start(raw[:], w1[a * 512 : (a + 1) * 512, :].rearrange("(p j) c -> p j c", j=PACK))
+            return raw
+
+        load_table(0)
+        for q in range(4):
+            nc.sync.dma_start(
+                w2_raw_scales[32 * q : 32 * q + 4, :].rearrange("p (a c) -> p a c", a=PASSES).bitcast(I32),
+                w2_scales[:, 4 * q : 4 * q + 4, :].rearrange("a q c -> q a c").bitcast(I32),
+            )
+        w2_raw = keep.tile([P, PASSES, 2 * H], U8, name="w2_raw", align_bytes=64)
+        nc.sync.dma_start(w2_raw[:].bitcast(I32), w2_words.rearrange("a p c -> p a c").bitcast(I32))
+        load_table(1)
+
+        picked_scales = keep.tile([P, S], U8, name="picked_scales", tag="w1_raw1", align_bytes=64)
+        nc.vector.tensor_copy(picked_scales[:], table_scales[:].indirect(idx[:]))
+        for a in range(PASSES):
+            first = SPARE + 4 * a
+            nc.sync.dma_start(v_scales[a][0 : P - first, :].bitcast(I32), picked_scales[first:P, :].bitcast(I32))
+
+        w1_raw = [load_w1(a) for a in range(PASSES)]
+        p1, p2, p3, p4, p5, p6 = [load_list(src, f"p{i + 1}") for i, src in enumerate((pos1, pos2, pos3, pos4, pos5, pos6))]
+        gains = keep.tile([P, PACK], F32, name="gains")
+        nc.sync.dma_start(gains[:], gain.rearrange("(p t) -> p t", t=PACK))
+
+        v_words = [[keep.tile([P, CHUNK], U32, name=f"v_words{a}_{c}", align_bytes=64) for c in range(CHUNKS)] for a in range(PASSES)]
+
+        def gather_words(a, c):
+            cols = CHUNK // 16
+            nc.vector.tensor_copy(v_words[a][c][:], table_words[a][:].bitcast(U32).indirect(idx[:, c * cols : (c + 1) * cols]))
+
+        for c in range(CHUNKS):
+            gather_words(0, c)
+        w2_codes = keep.tile([P, PASSES, 2 * H], U8, name="w2_codes", align_bytes=64)
+        w2_planes = keep.tile([P, PASSES, H], U8, name="w2_planes", align_bytes=64)
+        nc.vector.tensor_copy(
+            w2_codes[:].bitcast(U16).rearrange("p a (t m) -> p a t m", t=PACK),
+            w2_raw[:].bitcast(U16).rearrange("p a (m t) -> p a t m", t=PACK),
+        )
+        nc.vector.tensor_copy(
+            w2_planes[:].rearrange("p a (t m) -> p a t m", t=PACK),
+            w2_raw_scales[:].rearrange("p (a m t) -> p a t m", a=PASSES, t=PACK),
+        )
+
+        w1_codes = keep.tile([P, PASSES, H], U32, name="w1_codes", align_bytes=64)
+        w1_scales = keep.tile([P, PASSES, H], U8, name="w1_scales", align_bytes=64)
+        w1_bf = [keep.tile([P, H * PACK], BF16, name=f"w1_bf{a}", tag=f"w_bf{a}", align_bytes=64) for a in range(PASSES)]
+        for c in range(CHUNKS):
+            gather_words(1, c)
+        for a in range(PASSES):
+            nc.vector.tensor_copy(
+                w1_bf[a][:].rearrange("p (t m j) -> p m t j", t=PACK, j=PACK),
+                w1_raw[a][:].rearrange("p j (m t) -> p m t j", t=PACK),
+            )
+        for a in range(PASSES):
+            nc.vector.quantize_mx(out=w1_codes[:, a, :].bitcast(E4M3), scales=w1_scales[:, a, :], in_=w1_bf[a][:])
+
+        banks = [psum.tile([P, CHUNK], F32, name=f"bank{b}") for b in range(8)]
+
+        def w2_operand(a, t):
+            return w2_codes[:, a, 2 * P * t : 2 * P * (t + 1)].bitcast(E2M1), w2_planes[:, a, P * t : P * (t + 1)]
+
+        def style_tanh(t, c, th):
+            bank = banks[3 + c % 2] if t == 0 else banks[5 + (t * CHUNKS + c) % 3]
+            cols = slice(c * CHUNK, (c + 1) * CHUNK)
+            for a in range(PASSES):
+                nc.tensor.matmul_mx(
+                    out=bank[:],
+                    lhsT=w1_codes[:, a, P * t : P * (t + 1)].bitcast(E4M3),
+                    lhsT_scale=w1_scales[:, a, P * t : P * (t + 1)],
+                    rhs=v_words[a][c][:].bitcast(E4M3),
+                    rhs_scale=v_scales[a][:, cols],
+                    start=(a == 0),
+                    stop=(a == PASSES - 1),
+                )
+            nc.scalar.activation(th[:, cols], bank[:], ACT.Tanh)
+
+        def phase_transposed(t, c):
+            bank = banks[(t * CHUNKS + c) % 3]
+            for b in range(BLOCKS):
+                for a in range(PASSES):
+                    codes, plane = w2_operand(a, t)
+                    first = c * CHUNK + b * P
+                    nc.tensor.matmul_mx(
+                        out=bank[:, b * P : (b + 1) * P],
+                        lhsT=v_words[a][c][:, b * P : (b + 1) * P].bitcast(E4M3), lhsT_scale=v_scales[a][:, first : first + P],
+                        rhs=codes, rhs_scale=plane,
+                        start=(a == 0), stop=(a == PASSES - 1),
+                    )
+            whole = work.tile([P, CHUNK], U32, name="whole", bufs=3)
+            nc.scalar.activation(whole[:], bank[:], ACT.Copy, scale=STEP / TURN, bias=BIG_BITS)
+            scaled = work.tile([P, CHUNK], F32, name="scaled", bufs=3)
+            nc.scalar.activation(scaled[:], bank[:], ACT.Copy, scale=-STEP / TURN)
+            return whole, scaled
+
+        def sine_transposed(c, h, whole, scaled):
+            bank = banks[3 + c % 2]
+            for b in range(BLOCKS):
+                block = slice(b * P, (b + 1) * P)
+                terms = (whole[:, block].bitcast(F32), minus_big[:], scaled[:, block])
+                for i, term in enumerate(terms):
+                    nc.tensor.matmul(bank[:, block], term, identity[:], start=(i == 0), stop=(i == 2), is_transpose=True)
+            nc.scalar.activation(h[:, c * CHUNK : (c + 1) * CHUNK], bank[:], ACT.Sin, scale=-TURN / STEP)
+
+        a3 = keep.tile([P, PACK, P3], F32, name="a3")
+
+        def halves(n):
+            return [(slice(e * n // 2, (e + 1) * n // 2), slice(e * n // 32, (e + 1) * n // 32)) for e in range(2)]
+
+        def levels(t, h):
+            g1 = work.tile([P, P1], F32, name="g1", bufs=1)
+            g2 = work.tile([P, P1], F32, name="g2", bufs=1)
+            a1 = work.tile([P, P1], F32, name="a1")
+            nc.vector.tensor_copy(g1[:], h[:].indirect(p1[:]))
+            for cols, entries in halves(P1):
+                nc.vector.tensor_copy(g2[:, cols], h[:].indirect(p2[:, entries]))
+            for cols, entries in halves(P1):
+                nc.vector.tensor_tensor(a1[:, cols], g1[:, cols], g2[:, cols], ALU.max)
+            g3 = work.tile([P, P2], F32, name="g3", bufs=1)
+            g4 = work.tile([P, P2], F32, name="g4", bufs=1)
+            a2 = work.tile([P, P2], F32, name="a2")
+            nc.vector.tensor_copy(g3[:], a1[:].indirect(p3[:]))
+            for cols, entries in halves(P2):
+                nc.vector.tensor_copy(g4[:, cols], a1[:].indirect(p4[:, entries]))
+            for cols, entries in halves(P2):
+                nc.vector.scalar_tensor_tensor(a2[:, cols], g3[:, cols], gains[:, t : t + 1], g4[:, cols], ALU.mult, ALU.mult)
+            g5 = work.tile([P, P3], F32, name="g5", bufs=1)
+            for cols, entries in halves(P3):
+                nc.vector.tensor_copy(g5[:, cols], a2[:].indirect(p5[:, entries]))
+            for cols, entries in halves(P3):
+                nc.vector.tensor_tensor(a3[:, t, cols], a2[:].indirect(p6[:, entries]), g5[:, cols], ALU.add)
+
+        hs = [work.tile([P, S], F32, name=f"h{t}", tag="h", bufs=3) for t in range(PACK)]
+        ths = [work.tile([P, S], F32, name=f"th{t}", tag="th", bufs=2, align_bytes=64) for t in range(PACK)]
+
+        def finish(t, c):
+            style_tanh(t, c, ths[t])
+            cols = slice(c * CHUNK, (c + 1) * CHUNK)
+            nc.vector.tensor_tensor(hs[t][:, cols], hs[t][:, cols], ths[t][:, cols], ALU.add)
+
+        w3_codes = keep.tile([P, N], U32, name="w3_codes", align_bytes=64)
+        w3_scales = keep.tile([P, N], U8, name="w3_scales", align_bytes=64)
+
+        def prepare_w3():
+            raw = keep.tile([P, PACK, N], F32, name="w3_raw", tag="table1", align_bytes=64)
+            nc.sync.dma_start(raw[:], w3.rearrange("(p j) c -> p j c", j=PACK))
+            for g in range(2):
+                rounded = work.tile([P, 512 * PACK], BF16, name=f"w3_bf{g}", tag="th", bufs=2, align_bytes=64)
+                nc.scalar.copy(
+                    rounded[:].rearrange("p (t m j) -> p m t j", t=PACK, j=PACK),
+                    raw[:, :, g * 512 : (g + 1) * 512].rearrange("p j (m t) -> p m t j", t=PACK),
+                )
+                cols = slice(g * 512, (g + 1) * 512)
+                nc.vector.quantize_mx(out=w3_codes[:, cols].bitcast(E4M3), scales=w3_scales[:, cols], in_=rounded[:])
+
+        steps = [(t, c) for t in range(PACK) for c in range(CHUNKS)]
+        ahead = phase_transposed(*steps[0])
+        for i, (t, c) in enumerate(steps):
+            terms = ahead
+            last_of_slice = i + 1 == len(steps) or steps[i + 1][0] != t
+            if i + 1 < len(steps):
+                ahead = phase_transposed(*steps[i + 1])
+            sine_transposed(c, hs[t], *terms)
+            if last_of_slice:
+                for late in range(CHUNKS):
+                    finish(t, late)
+                if t == PACK - 1:
+                    prepare_w3()
+                levels(t, hs[t])
+
+        a3_bf = keep.tile([P, P3 * PACK], BF16, name="a3_bf", align_bytes=64)
+        nc.vector.tensor_copy(a3_bf[:].rearrange("p (j t) -> p j t", t=PACK), a3[:].rearrange("p t j -> p j t"))
+        a3_codes = keep.tile([P, P3], U32, name="a3_codes", align_bytes=64)
+        a3_scales = keep.tile([P, P3], U8, name="a3_scales", align_bytes=64)
+        nc.vector.quantize_mx(out=a3_codes[:].bitcast(E4M3), scales=a3_scales[:], in_=a3_bf[:])
+
+        y_scales = keep.tile([P, 2, P3], U8, name="y_scales", align_bytes=64)
+        for g in range(2):
+            y = keep.tile([P, PACK, P3], F32, name=f"y{g}")
+            for half in range(2):
+                bank = banks[2 * g + half][:].rearrange("p (e j) -> p e j", e=2)
+                for e in range(2):
+                    cols = slice(g * 512 + (2 * half + e) * P, g * 512 + (2 * half + e + 1) * P)
+                    nc.tensor.matmul_mx(
+                        out=bank[:, e, :], lhsT=w3_codes[:, cols].bitcast(E4M3), lhsT_scale=w3_scales[:, cols],
+                        rhs=a3_codes[:].bitcast(E4M3), rhs_scale=a3_scales[:], start=True, stop=True,
+                    )
+                if (g, half) == (0, 1):
+                    nc.vector.tensor_copy(y[:, 2 * half : 2 * half + 2, :], bank)
+                else:
+                    nc.scalar.copy(y[:, 2 * half : 2 * half + 2, :], bank)
+            nc.sync.dma_start(out_0[g * 512 : (g + 1) * 512, :].rearrange("(p u) j -> p u j", u=PACK), y[:])
+            y_bf = keep.tile([P, P3 * PACK], BF16, name=f"y_bf{g}", align_bytes=64)
+            nc.vector.tensor_copy(y_bf[:].rearrange("p (j u) -> p j u", u=PACK), y[:].rearrange("p u j -> p j u"))
+            y_codes = keep.tile([P, P3], U32, name=f"y_codes{g}", align_bytes=64)
+            nc.vector.quantize_mx(out=y_codes[:].bitcast(E4M3), scales=y_scales[:, g, :], in_=y_bf[:])
+            nc.sync.dma_start(out_1[g].rearrange("p m t -> p (m t)").bitcast(I32), y_codes[:].bitcast(I32))
+        for q in range(4):
+            nc.scalar.dma_start(
+                out_2[:, 4 * q : 4 * q + 4, :].rearrange("g q m -> q g m").bitcast(I32),
+                y_scales[32 * q : 32 * q + 4, :, :].bitcast(I32),
+            )

@@ -57,6 +57,8 @@ def tile_list_olympiad_paper_features_kernel(
             nc.gpsimd.memset(v_scales[a][:].bitcast(I32), 0)
         identity = keep.tile([P, P], F32, name="identity")
         make_identity(nc, identity[:])
+        warm_out = keep.tile([P, 1], F32, name="warm_out")
+        nc.scalar.activation(warm_out[:], identity[:, 0:1], ACT.Silu)
         minus_big = keep.tile([P, P], F32, name="minus_big")
         nc.gpsimd.memset(minus_big[:], -BIG)
 
@@ -122,11 +124,12 @@ def tile_list_olympiad_paper_features_kernel(
         for c in range(CHUNKS):
             gather_words(1, c)
         for a in range(PASSES):
-            nc.vector.tensor_copy(
+            nc.scalar.copy(
                 w1_bf[a][:].rearrange("p (t m j) -> p m t j", t=PACK, j=PACK),
                 w1_raw[a][:].rearrange("p j (m t) -> p m t j", t=PACK),
             )
-        for a in range(PASSES):
+
+        def quantise_w1(a):
             nc.vector.quantize_mx(out=w1_codes[:, a, :].bitcast(E4M3), scales=w1_scales[:, a, :], in_=w1_bf[a][:])
 
         banks = [psum.tile([P, CHUNK], F32, name=f"bank{b}") for b in range(8)]
@@ -135,7 +138,7 @@ def tile_list_olympiad_paper_features_kernel(
             return w2_codes[:, a, 2 * P * t : 2 * P * (t + 1)].bitcast(E2M1), w2_planes[:, a, P * t : P * (t + 1)]
 
         def style_tanh(t, c, th):
-            bank = banks[3 + c % 2] if t == 0 else banks[5 + (t * CHUNKS + c) % 3]
+            bank = banks[4 + c]
             cols = slice(c * CHUNK, (c + 1) * CHUNK)
             for a in range(PASSES):
                 nc.tensor.matmul_mx(
@@ -149,8 +152,24 @@ def tile_list_olympiad_paper_features_kernel(
                 )
             nc.scalar.activation(th[:, cols], bank[:], ACT.Tanh)
 
+        def sine_direct(t, c, h):
+            bank = banks[4 + c]
+            cols = slice(c * CHUNK, (c + 1) * CHUNK)
+            for a in range(PASSES):
+                codes, plane = w2_operand(a, t)
+                nc.tensor.matmul_mx(
+                    out=bank[:], lhsT=codes, lhsT_scale=plane,
+                    rhs=v_words[a][c][:].bitcast(E4M3), rhs_scale=v_scales[a][:, cols],
+                    start=(a == 0), stop=(a == PASSES - 1),
+                )
+            turns = keep.tile([P, CHUNK], I32, name=f"turns{c}", tag="w_bf1" if c == 2 else "turns", align_bytes=64)
+            nc.vector.tensor_scalar(turns[:], bank[:], 1.0 / TURN, None, ALU.mult)
+            rest = keep.tile([P, CHUNK], F32, name=f"rest{c}")
+            nc.vector.scalar_tensor_tensor(rest[:], bank[:], 1.0 / TURN, turns[:], ALU.mult, ALU.subtract)
+            nc.scalar.activation(h[:, cols], rest[:], ACT.Sin, scale=TURN)
+
         def phase_transposed(t, c):
-            bank = banks[(t * CHUNKS + c) % 3]
+            bank = banks[c % 2]
             for b in range(BLOCKS):
                 for a in range(PASSES):
                     codes, plane = w2_operand(a, t)
@@ -168,7 +187,7 @@ def tile_list_olympiad_paper_features_kernel(
             return whole, scaled
 
         def sine_transposed(c, h, whole, scaled):
-            bank = banks[3 + c % 2]
+            bank = banks[2 + c % 2]
             for b in range(BLOCKS):
                 block = slice(b * P, (b + 1) * P)
                 terms = (whole[:, block].bitcast(F32), minus_big[:], scaled[:, block])
@@ -204,7 +223,8 @@ def tile_list_olympiad_paper_features_kernel(
             for cols, entries in halves(P3):
                 nc.vector.tensor_tensor(a3[:, t, cols], a2[:].indirect(p6[:, entries]), g5[:, cols], ALU.add)
 
-        hs = [work.tile([P, S], F32, name=f"h{t}", tag="h", bufs=3) for t in range(PACK)]
+        hs = [keep.tile([P, S], F32, name="h0", tag="w1_raw1", align_bytes=64)]
+        hs = hs + [work.tile([P, S], F32, name=f"h{t}", tag="h", bufs=2) for t in range(1, PACK)]
         ths = [work.tile([P, S], F32, name=f"th{t}", tag="th", bufs=2, align_bytes=64) for t in range(PACK)]
 
         def finish(t, c):
@@ -227,17 +247,25 @@ def tile_list_olympiad_paper_features_kernel(
                 cols = slice(g * 512, (g + 1) * 512)
                 nc.vector.quantize_mx(out=w3_codes[:, cols].bitcast(E4M3), scales=w3_scales[:, cols], in_=rounded[:])
 
-        steps = [(t, c) for t in range(PACK) for c in range(CHUNKS)]
+        for c in range(CHUNKS):
+            if c == 2:
+                quantise_w1(1)
+            sine_direct(0, c, hs[0])
+            if c == 0:
+                quantise_w1(0)
+        for c in range(CHUNKS):
+            finish(0, c)
+        levels(0, hs[0])
+
+        steps = [(t, c) for t in range(1, PACK) for c in range(CHUNKS)]
         ahead = phase_transposed(*steps[0])
         for i, (t, c) in enumerate(steps):
             terms = ahead
-            last_of_slice = i + 1 == len(steps) or steps[i + 1][0] != t
             if i + 1 < len(steps):
                 ahead = phase_transposed(*steps[i + 1])
             sine_transposed(c, hs[t], *terms)
-            if last_of_slice:
-                for late in range(CHUNKS):
-                    finish(t, late)
+            finish(t, c)
+            if c == CHUNKS - 1:
                 if t == PACK - 1:
                     prepare_w3()
                 levels(t, hs[t])

@@ -230,7 +230,8 @@ def tile_list_olympiad_paper_features_kernel(
         def finish(t, c):
             style_tanh(t, c, ths[t])
             cols = slice(c * CHUNK, (c + 1) * CHUNK)
-            nc.vector.tensor_tensor(hs[t][:, cols], hs[t][:, cols], ths[t][:, cols], ALU.add)
+            engine = nc.vector if t == 0 else nc.gpsimd
+            engine.tensor_tensor(hs[t][:, cols], hs[t][:, cols], ths[t][:, cols], ALU.add)
 
         w3_codes = keep.tile([P, N], U32, name="w3_codes", align_bytes=64)
         w3_scales = keep.tile([P, N], U8, name="w3_scales", align_bytes=64)

@@ -46,7 +46,7 @@ def tile_list_olympiad_paper_features_kernel(
             nc.sync.dma_start(tile[:], src)
             return tile
 
-        table_scales = keep.tile([P, T], U8, name="table_scales", tag="w1_raw0", align_bytes=64)
+        table_scales = keep.tile([P, T], U8, name="table_scales", tag="w1_raw", align_bytes=64)
         w2_raw_scales = keep.tile([P, PASSES * H], U8, name="w2_raw_scales", align_bytes=64)
         nc.gpsimd.memset(w2_raw_scales[:].bitcast(I32), 0)
         for q in range(4):
@@ -73,11 +73,6 @@ def tile_list_olympiad_paper_features_kernel(
         def load_table(a):
             nc.sync.dma_start(table_words[a][:], tab_words[a].rearrange("p t i -> p (t i)").bitcast(I32))
 
-        def load_w1(a):
-            raw = keep.tile([P, PACK, H], F32, name=f"w1_raw{a}", tag=f"w1_raw{a}", align_bytes=64)
-            nc.sync.dma_start(raw[:], w1[a * 512 : (a + 1) * 512, :].rearrange("(p j) c -> p j c", j=PACK))
-            return raw
-
         load_table(0)
         for q in range(4):
             nc.sync.dma_start(
@@ -88,13 +83,15 @@ def tile_list_olympiad_paper_features_kernel(
         nc.sync.dma_start(w2_raw[:].bitcast(I32), w2_words.rearrange("a p c -> p a c").bitcast(I32))
         load_table(1)
 
-        picked_scales = keep.tile([P, S], U8, name="picked_scales", tag="w1_raw1", align_bytes=64)
+        picked_scales = keep.tile([P, S], U8, name="picked_scales", align_bytes=64)
         nc.vector.tensor_copy(picked_scales[:], table_scales[:].indirect(idx[:]))
         for a in range(PASSES):
             first = SPARE + 4 * a
             nc.sync.dma_start(v_scales[a][0 : P - first, :].bitcast(I32), picked_scales[first:P, :].bitcast(I32))
 
-        w1_raw = [load_w1(a) for a in range(PASSES)]
+        w1_raw = keep.tile([P, PASSES, PACK * H], F32, name="w1_raw", tag="w1_raw", align_bytes=64)
+        for a in range(PASSES):
+            nc.sync.dma_start(w1_raw[:, a, :], w1[a * 512 : (a + 1) * 512, :].rearrange("(p j) c -> p (j c)", j=PACK))
         p1, p2, p3, p4, p5, p6 = [load_list(src, f"p{i + 1}") for i, src in enumerate((pos1, pos2, pos3, pos4, pos5, pos6))]
         gains = keep.tile([P, PACK], F32, name="gains")
         nc.sync.dma_start(gains[:], gain.rearrange("(p t) -> p t", t=PACK))
@@ -113,24 +110,27 @@ def tile_list_olympiad_paper_features_kernel(
             w2_codes[:].bitcast(U16).rearrange("p a (t m) -> p a t m", t=PACK),
             w2_raw[:].bitcast(U16).rearrange("p a (m t) -> p a t m", t=PACK),
         )
-        nc.vector.tensor_copy(
+        nc.gpsimd.tensor_copy(
             w2_planes[:].rearrange("p a (t m) -> p a t m", t=PACK),
             w2_raw_scales[:].rearrange("p (a m t) -> p a t m", a=PASSES, t=PACK),
         )
 
-        w1_codes = keep.tile([P, PASSES, H], U32, name="w1_codes", align_bytes=64)
-        w1_scales = keep.tile([P, PASSES, H], U8, name="w1_scales", align_bytes=64)
-        w1_bf = [keep.tile([P, H * PACK], BF16, name=f"w1_bf{a}", tag=f"w_bf{a}", align_bytes=64) for a in range(PASSES)]
         for c in range(CHUNKS):
             gather_words(1, c)
-        for a in range(PASSES):
-            nc.scalar.copy(
-                w1_bf[a][:].rearrange("p (t m j) -> p m t j", t=PACK, j=PACK),
-                w1_raw[a][:].rearrange("p j (m t) -> p m t j", t=PACK),
-            )
 
-        def quantise_w1(a):
-            nc.vector.quantize_mx(out=w1_codes[:, a, :].bitcast(E4M3), scales=w1_scales[:, a, :], in_=w1_bf[a][:])
+        def prepare_w1(first, count, tag):
+            width = count * P
+            rounded = keep.tile([P, PASSES, width * PACK], BF16, name=f"w1_bf{first}", tag=tag, align_bytes=64)
+            codes = keep.tile([P, PASSES, width], U32, name=f"w1_codes{first}", align_bytes=64)
+            planes = keep.tile([P, PASSES, width], U8, name=f"w1_planes{first}", align_bytes=64)
+            for a in range(PASSES):
+                nc.scalar.copy(
+                    rounded[:, a, :].rearrange("p (t m j) -> p m t j", t=count, j=PACK),
+                    w1_raw[:, a, :].rearrange("p (j m t) -> p m t j", j=PACK, t=PACK)[:, :, first : first + count, :],
+                )
+            for a in range(PASSES):
+                nc.vector.quantize_mx(out=codes[:, a, :].bitcast(E4M3), scales=planes[:, a, :], in_=rounded[:, a, :])
+            return [(codes[:, :, e * P : (e + 1) * P], planes[:, :, e * P : (e + 1) * P]) for e in range(count)]
 
         banks = [psum.tile([P, CHUNK], F32, name=f"bank{b}") for b in range(8)]
 
@@ -138,13 +138,13 @@ def tile_list_olympiad_paper_features_kernel(
             return w2_codes[:, a, 2 * P * t : 2 * P * (t + 1)].bitcast(E2M1), w2_planes[:, a, P * t : P * (t + 1)]
 
         def style_tanh(t, c, th):
-            bank = banks[4 + c]
+            bank = banks[4 + c] if t == 0 else banks[2 + c % 2]
             cols = slice(c * CHUNK, (c + 1) * CHUNK)
             for a in range(PASSES):
                 nc.tensor.matmul_mx(
                     out=bank[:],
-                    lhsT=w1_codes[:, a, P * t : P * (t + 1)].bitcast(E4M3),
-                    lhsT_scale=w1_scales[:, a, P * t : P * (t + 1)],
+                    lhsT=w1_q[t][0][:, a, :].bitcast(E4M3),
+                    lhsT_scale=w1_q[t][1][:, a, :],
                     rhs=v_words[a][c][:].bitcast(E4M3),
                     rhs_scale=v_scales[a][:, cols],
                     start=(a == 0),
@@ -162,7 +162,7 @@ def tile_list_olympiad_paper_features_kernel(
                     rhs=v_words[a][c][:].bitcast(E4M3), rhs_scale=v_scales[a][:, cols],
                     start=(a == 0), stop=(a == PASSES - 1),
                 )
-            turns = keep.tile([P, CHUNK], I32, name=f"turns{c}", tag="w_bf1" if c == 2 else "turns", align_bytes=64)
+            turns = keep.tile([P, CHUNK], I32, name=f"turns{c}", tag="turns", align_bytes=64)
             nc.vector.tensor_scalar(turns[:], bank[:], 1.0 / TURN, None, ALU.mult)
             rest = keep.tile([P, CHUNK], F32, name=f"rest{c}")
             nc.vector.scalar_tensor_tensor(rest[:], bank[:], 1.0 / TURN, turns[:], ALU.mult, ALU.subtract)
@@ -180,14 +180,14 @@ def tile_list_olympiad_paper_features_kernel(
                         rhs=codes, rhs_scale=plane,
                         start=(a == 0), stop=(a == PASSES - 1),
                     )
-            whole = work.tile([P, CHUNK], U32, name="whole", bufs=3)
+            whole = work.tile([P, CHUNK], U32, name="whole")
             nc.scalar.activation(whole[:], bank[:], ACT.Copy, scale=STEP / TURN, bias=BIG_BITS)
-            scaled = work.tile([P, CHUNK], F32, name="scaled", bufs=3)
+            scaled = work.tile([P, CHUNK], F32, name="scaled")
             nc.scalar.activation(scaled[:], bank[:], ACT.Copy, scale=-STEP / TURN)
             return whole, scaled
 
-        def sine_transposed(c, h, whole, scaled):
-            bank = banks[2 + c % 2]
+        def sine_transposed(t, c, h, whole, scaled):
+            bank = banks[2] if t == 0 else banks[5 + c % 2]
             for b in range(BLOCKS):
                 block = slice(b * P, (b + 1) * P)
                 terms = (whole[:, block].bitcast(F32), minus_big[:], scaled[:, block])
@@ -223,14 +223,14 @@ def tile_list_olympiad_paper_features_kernel(
             for cols, entries in halves(P3):
                 nc.vector.tensor_tensor(a3[:, t, cols], a2[:].indirect(p6[:, entries]), g5[:, cols], ALU.add)
 
-        hs = [keep.tile([P, S], F32, name="h0", tag="w1_raw1", align_bytes=64)]
-        hs = hs + [work.tile([P, S], F32, name=f"h{t}", tag="h", bufs=2) for t in range(1, PACK)]
-        ths = [work.tile([P, S], F32, name=f"th{t}", tag="th", bufs=2, align_bytes=64) for t in range(PACK)]
+        hs = [keep.tile([P, S], F32, name="h0")]
+        hs = hs + [work.tile([P, S], F32, name=f"h{t}", bufs=1) for t in range(1, PACK)]
+        ths = [work.tile([P, S], F32, name=f"th{t}", bufs=1, align_bytes=64) for t in range(PACK)]
 
         def finish(t, c):
             style_tanh(t, c, ths[t])
             cols = slice(c * CHUNK, (c + 1) * CHUNK)
-            engine = nc.vector if t == 0 else nc.gpsimd
+            engine = nc.vector if c == CHUNKS - 1 else nc.gpsimd
             engine.tensor_tensor(hs[t][:, cols], hs[t][:, cols], ths[t][:, cols], ALU.add)
 
         w3_codes = keep.tile([P, N], U32, name="w3_codes", align_bytes=64)
@@ -240,22 +240,22 @@ def tile_list_olympiad_paper_features_kernel(
             raw = keep.tile([P, PACK, N], F32, name="w3_raw", tag="table1", align_bytes=64)
             nc.sync.dma_start(raw[:], w3.rearrange("(p j) c -> p j c", j=PACK))
             for g in range(2):
-                rounded = work.tile([P, 512 * PACK], BF16, name=f"w3_bf{g}", tag="th", bufs=2, align_bytes=64)
+                rounded = ths[3][:].bitcast(BF16)[:, g * 512 * PACK : (g + 1) * 512 * PACK]
                 nc.scalar.copy(
-                    rounded[:].rearrange("p (t m j) -> p m t j", t=PACK, j=PACK),
+                    rounded.rearrange("p (t m j) -> p m t j", t=PACK, j=PACK),
                     raw[:, :, g * 512 : (g + 1) * 512].rearrange("p j (m t) -> p m t j", t=PACK),
                 )
                 cols = slice(g * 512, (g + 1) * 512)
-                nc.vector.quantize_mx(out=w3_codes[:, cols].bitcast(E4M3), scales=w3_scales[:, cols], in_=rounded[:])
+                nc.vector.quantize_mx(out=w3_codes[:, cols].bitcast(E4M3), scales=w3_scales[:, cols], in_=rounded)
 
-        for c in range(CHUNKS):
-            if c == 2:
-                quantise_w1(1)
-            sine_direct(0, c, hs[0])
-            if c == 0:
-                quantise_w1(0)
+        sine_transposed(0, 0, hs[0], *phase_transposed(0, 0))
+        w1_q = prepare_w1(0, 1, "turns")
+        sine_direct(0, 1, hs[0])
         for c in range(CHUNKS):
             finish(0, c)
+            if c + 2 < CHUNKS:
+                sine_direct(0, c + 2, hs[0])
+        w1_q.extend(prepare_w1(1, PACK - 1, "w1_bf"))
         levels(0, hs[0])
 
         steps = [(t, c) for t in range(1, PACK) for c in range(CHUNKS)]
@@ -264,7 +264,7 @@ def tile_list_olympiad_paper_features_kernel(
             terms = ahead
             if i + 1 < len(steps):
                 ahead = phase_transposed(*steps[i + 1])
-            sine_transposed(c, hs[t], *terms)
+            sine_transposed(t, c, hs[t], *terms)
             finish(t, c)
             if c == CHUNKS - 1:
                 if t == PACK - 1:
@@ -278,8 +278,8 @@ def tile_list_olympiad_paper_features_kernel(
         nc.vector.quantize_mx(out=a3_codes[:].bitcast(E4M3), scales=a3_scales[:], in_=a3_bf[:])
 
         y_scales = keep.tile([P, 2, P3], U8, name="y_scales", align_bytes=64)
+        ys = [keep.tile([P, PACK, P3], F32, name=f"y{g}") for g in range(2)]
         for g in range(2):
-            y = keep.tile([P, PACK, P3], F32, name=f"y{g}")
             for half in range(2):
                 bank = banks[2 * g + half][:].rearrange("p (e j) -> p e j", e=2)
                 for e in range(2):
@@ -288,13 +288,13 @@ def tile_list_olympiad_paper_features_kernel(
                         out=bank[:, e, :], lhsT=w3_codes[:, cols].bitcast(E4M3), lhsT_scale=w3_scales[:, cols],
                         rhs=a3_codes[:].bitcast(E4M3), rhs_scale=a3_scales[:], start=True, stop=True,
                     )
-                if (g, half) == (0, 1):
-                    nc.vector.tensor_copy(y[:, 2 * half : 2 * half + 2, :], bank)
-                else:
-                    nc.scalar.copy(y[:, 2 * half : 2 * half + 2, :], bank)
-            nc.sync.dma_start(out_0[g * 512 : (g + 1) * 512, :].rearrange("(p u) j -> p u j", u=PACK), y[:])
+                copy = nc.scalar.copy if half == 0 else nc.vector.tensor_copy
+                copy(ys[g][:, 2 * half : 2 * half + 2, :], bank)
+            nc.sync.dma_start(out_0[g * 512 : (g + 1) * 512, :].rearrange("(p u) j -> p u j", u=PACK), ys[g][:])
+        for g in range(2):
             y_bf = keep.tile([P, P3 * PACK], BF16, name=f"y_bf{g}", align_bytes=64)
-            nc.vector.tensor_copy(y_bf[:].rearrange("p (j u) -> p j u", u=PACK), y[:].rearrange("p u j -> p j u"))
+            copy = nc.vector.tensor_copy if g == 0 else nc.scalar.copy
+            copy(y_bf[:].rearrange("p (j u) -> p j u", u=PACK), ys[g][:].rearrange("p u j -> p j u"))
             y_codes = keep.tile([P, P3], U32, name=f"y_codes{g}", align_bytes=64)
             nc.vector.quantize_mx(out=y_codes[:].bitcast(E4M3), scales=y_scales[:, g, :], in_=y_bf[:])
             nc.sync.dma_start(out_1[g].rearrange("p m t -> p (m t)").bitcast(I32), y_codes[:].bitcast(I32))

import math
from contextlib import ExitStack

import concourse.mybir as mybir
from concourse.masks import make_identity

K, H, T, S, P1, P2, P3, N = 1024, 512, 4096, 2048, 1024, 512, 256, 1024
FLOPS = 2 * (2 * K * H * S + H * N * P3)

F32 = mybir.dt.float32
BF16 = mybir.dt.bfloat16
I32 = mybir.dt.int32
U32 = mybir.dt.uint32
U16 = mybir.dt.uint16
U8 = mybir.dt.uint8
E4M3 = mybir.dt.float8_e4m3fn_x4
E2M1 = mybir.dt.float4_e2m1fn_x4
ALU = mybir.AluOpType
ACT = mybir.ActivationFunctionType

P = 128
PACK = 4
PASSES = K // (P * PACK)
CHUNK = 512
CHUNKS = S // CHUNK
BLOCKS = CHUNK // P
TURN = 2.0 * math.pi
BIG = 1.5 * 2.0**23
BIG_BITS = float(0x4B400000)
STEP = 128.0
SPARE = 32 - 4 * PASSES


def tile_list_olympiad_paper_features_kernel(
    tc, tab_words, tab_scales, offs, w1, w2_words, w2_scales, pos1, pos2, pos3, pos4, pos5, pos6, gain, w3, out_0, out_1, out_2
):
    nc = tc.nc
    with ExitStack() as ctx:
        lists = ctx.enter_context(tc.tile_pool(name="lists", bufs=1))
        keep = ctx.enter_context(tc.tile_pool(name="keep", bufs=1))
        work = ctx.enter_context(tc.tile_pool(name="work", bufs=2))
        psum = ctx.enter_context(tc.psum_pool(name="psum", bufs=1))

        def load_list(src, name):
            tile = lists.tile(list(src.shape), U16, name=name)
            nc.sync.dma_start(tile[:], src)
            return tile

        table_scales = keep.tile([P, T], U8, name="table_scales", tag="w1_raw", align_bytes=64)
        w2_raw_scales = keep.tile([P, PASSES * H], U8, name="w2_raw_scales", align_bytes=64)
        nc.gpsimd.memset(w2_raw_scales[:].bitcast(I32), 0)
        for q in range(4):
            engine = nc.vector if q % 2 == 0 else nc.gpsimd
            engine.memset(table_scales[32 * q : 32 * q + SPARE, :].bitcast(I32), 0)
        v_scales = [keep.tile([P, S], U8, name=f"v_scales{a}", align_bytes=64) for a in range(PASSES)]
        for a in range(PASSES):
            nc.gpsimd.memset(v_scales[a][:].bitcast(I32), 0)
        identity = keep.tile([P, P], F32, name="identity")
        make_identity(nc, identity[:])
        warm_out = keep.tile([P, 1], F32, name="warm_out")
        nc.scalar.activation(warm_out[:], identity[:, 0:1], ACT.Silu)
        minus_big = keep.tile([P, P], F32, name="minus_big")
        nc.gpsimd.memset(minus_big[:], -BIG)

        idx = load_list(offs, "idx")
        for q in range(4):
            nc.sync.dma_start(
                table_scales[32 * q + SPARE : 32 * (q + 1), :].bitcast(I32),
                tab_scales[:, 4 * q : 4 * q + 4, :].bitcast(I32),
            )
        table_words = [keep.tile([P, T], I32, name=f"table_words{a}", tag=f"table{a}", align_bytes=64) for a in range(PASSES)]

        def load_table(a):
            nc.sync.dma_start(table_words[a][:], tab_words[a].rearrange("p t i -> p (t i)").bitcast(I32))

        load_table(0)
        for q in range(4):
            nc.sync.dma_start(
                w2_raw_scales[32 * q : 32 * q + 4, :].rearrange("p (a c) -> p a c", a=PASSES).bitcast(I32),
                w2_scales[:, 4 * q : 4 * q + 4, :].rearrange("a q c -> q a c").bitcast(I32),
            )
        w2_raw = keep.tile([P, PASSES, 2 * H], U8, name="w2_raw", align_bytes=64)
        nc.sync.dma_start(w2_raw[:].bitcast(I32), w2_words.rearrange("a p c -> p a c").bitcast(I32))
        load_table(1)

        picked_scales = keep.tile([P, S], U8, name="picked_scales", align_bytes=64)
        nc.vector.tensor_copy(picked_scales[:], table_scales[:].indirect(idx[:]))
        for a in range(PASSES):
            first = SPARE + 4 * a
            nc.sync.dma_start(v_scales[a][0 : P - first, :].bitcast(I32), picked_scales[first:P, :].bitcast(I32))

        w1_raw = keep.tile([P, PASSES, PACK * H], F32, name="w1_raw", tag="w1_raw", align_bytes=64)
        for a in range(PASSES):
            nc.sync.dma_start(w1_raw[:, a, :], w1[a * 512 : (a + 1) * 512, :].rearrange("(p j) c -> p (j c)", j=PACK))
        p1, p2, p3, p4, p5, p6 = [load_list(src, f"p{i + 1}") for i, src in enumerate((pos1, pos2, pos3, pos4, pos5, pos6))]
        gains = keep.tile([P, PACK], F32, name="gains")
        nc.sync.dma_start(gains[:], gain.rearrange("(p t) -> p t", t=PACK))

        v_words = [[keep.tile([P, CHUNK], U32, name=f"v_words{a}_{c}", align_bytes=64) for c in range(CHUNKS)] for a in range(PASSES)]

        def gather_words(a, c):
            cols = CHUNK // 16
            nc.vector.tensor_copy(v_words[a][c][:], table_words[a][:].bitcast(U32).indirect(idx[:, c * cols : (c + 1) * cols]))

        for c in range(CHUNKS):
            gather_words(0, c)
        w2_codes = keep.tile([P, PASSES, 2 * H], U8, name="w2_codes", align_bytes=64)
        w2_planes = keep.tile([P, PASSES, H], U8, name="w2_planes", align_bytes=64)
        nc.vector.tensor_copy(
            w2_codes[:].bitcast(U16).rearrange("p a (t m) -> p a t m", t=PACK),
            w2_raw[:].bitcast(U16).rearrange("p a (m t) -> p a t m", t=PACK),
        )
        nc.gpsimd.tensor_copy(
            w2_planes[:].rearrange("p a (t m) -> p a t m", t=PACK),
            w2_raw_scales[:].rearrange("p (a m t) -> p a t m", a=PASSES, t=PACK),
        )

        for c in range(CHUNKS):
            gather_words(1, c)

        def prepare_w1(first, count, tag):
            width = count * P
            rounded = keep.tile([P, PASSES, width * PACK], BF16, name=f"w1_bf{first}", tag=tag, align_bytes=64)
            codes = keep.tile([P, PASSES, width], U32, name=f"w1_codes{first}", align_bytes=64)
            planes = keep.tile([P, PASSES, width], U8, name=f"w1_planes{first}", align_bytes=64)
            for a in range(PASSES):
                nc.scalar.copy(
                    rounded[:, a, :].rearrange("p (t m j) -> p m t j", t=count, j=PACK),
                    w1_raw[:, a, :].rearrange("p (j m t) -> p m t j", j=PACK, t=PACK)[:, :, first : first + count, :],
                )
            for a in range(PASSES):
                nc.vector.quantize_mx(out=codes[:, a, :].bitcast(E4M3), scales=planes[:, a, :], in_=rounded[:, a, :])
            return [(codes[:, :, e * P : (e + 1) * P], planes[:, :, e * P : (e + 1) * P]) for e in range(count)]

        banks = [psum.tile([P, CHUNK], F32, name=f"bank{b}") for b in range(8)]

        def w2_operand(a, t):
            return w2_codes[:, a, 2 * P * t : 2 * P * (t + 1)].bitcast(E2M1), w2_planes[:, a, P * t : P * (t + 1)]

        def style_tanh(t, c, th):
            bank = banks[4 + c] if t == 0 else banks[2 + c % 2]
            cols = slice(c * CHUNK, (c + 1) * CHUNK)
            for a in range(PASSES):
                nc.tensor.matmul_mx(
                    out=bank[:],
                    lhsT=w1_q[t][0][:, a, :].bitcast(E4M3),
                    lhsT_scale=w1_q[t][1][:, a, :],
                    rhs=v_words[a][c][:].bitcast(E4M3),
                    rhs_scale=v_scales[a][:, cols],
                    start=(a == 0),
                    stop=(a == PASSES - 1),
                )
            nc.scalar.activation(th[:, cols], bank[:], ACT.Tanh)

        def sine_direct(t, c, h):
            bank = banks[4 + c]
            cols = slice(c * CHUNK, (c + 1) * CHUNK)
            for a in range(PASSES):
                codes, plane = w2_operand(a, t)
                nc.tensor.matmul_mx(
                    out=bank[:], lhsT=codes, lhsT_scale=plane,
                    rhs=v_words[a][c][:].bitcast(E4M3), rhs_scale=v_scales[a][:, cols],
                    start=(a == 0), stop=(a == PASSES - 1),
                )
            turns = keep.tile([P, CHUNK], I32, name=f"turns{c}", tag="turns", align_bytes=64)
            nc.vector.tensor_scalar(turns[:], bank[:], 1.0 / TURN, None, ALU.mult)
            rest = keep.tile([P, CHUNK], F32, name=f"rest{c}")
            nc.vector.scalar_tensor_tensor(rest[:], bank[:], 1.0 / TURN, turns[:], ALU.mult, ALU.subtract)
            nc.scalar.activation(h[:, cols], rest[:], ACT.Sin, scale=TURN)

        def phase_transposed(t, c):
            bank = banks[c % 2]
            for b in range(BLOCKS):
                for a in range(PASSES):
                    codes, plane = w2_operand(a, t)
                    first = c * CHUNK + b * P
                    nc.tensor.matmul_mx(
                        out=bank[:, b * P : (b + 1) * P],
                        lhsT=v_words[a][c][:, b * P : (b + 1) * P].bitcast(E4M3), lhsT_scale=v_scales[a][:, first : first + P],
                        rhs=codes, rhs_scale=plane,
                        start=(a == 0), stop=(a == PASSES - 1),
                    )
            whole = work.tile([P, CHUNK], U32, name="whole")
            nc.scalar.activation(whole[:], bank[:], ACT.Copy, scale=STEP / TURN, bias=BIG_BITS)
            scaled = work.tile([P, CHUNK], F32, name="scaled")
            nc.scalar.activation(scaled[:], bank[:], ACT.Copy, scale=-STEP / TURN)
            return whole, scaled

        def sine_transposed(t, c, h, whole, scaled):
            bank = banks[2] if t == 0 else banks[5 + c % 2]
            for b in range(BLOCKS):
                block = slice(b * P, (b + 1) * P)
                terms = (whole[:, block].bitcast(F32), minus_big[:], scaled[:, block])
                for i, term in enumerate(terms):
                    nc.tensor.matmul(bank[:, block], term, identity[:], start=(i == 0), stop=(i == 2), is_transpose=True)
            nc.scalar.activation(h[:, c * CHUNK : (c + 1) * CHUNK], bank[:], ACT.Sin, scale=-TURN / STEP)

        a3 = keep.tile([P, PACK, P3], F32, name="a3")

        def halves(n):
            return [(slice(e * n // 2, (e + 1) * n // 2), slice(e * n // 32, (e + 1) * n // 32)) for e in range(2)]

        def levels(t, h):
            g1 = work.tile([P, P1], F32, name="g1", bufs=1)
            g2 = work.tile([P, P1], F32, name="g2", bufs=1)
            a1 = work.tile([P, P1], F32, name="a1")
            nc.vector.tensor_copy(g1[:], h[:].indirect(p1[:]))
            for cols, entries in halves(P1):
                nc.vector.tensor_copy(g2[:, cols], h[:].indirect(p2[:, entries]))
            for cols, entries in halves(P1):
                nc.vector.tensor_tensor(a1[:, cols], g1[:, cols], g2[:, cols], ALU.max)
            g3 = work.tile([P, P2], F32, name="g3", bufs=1)
            g4 = work.tile([P, P2], F32, name="g4", bufs=1)
            a2 = work.tile([P, P2], F32, name="a2")
            nc.vector.tensor_copy(g3[:], a1[:].indirect(p3[:]))
            for cols, entries in halves(P2):
                nc.vector.tensor_copy(g4[:, cols], a1[:].indirect(p4[:, entries]))
            for cols, entries in halves(P2):
                nc.vector.scalar_tensor_tensor(a2[:, cols], g3[:, cols], gains[:, t : t + 1], g4[:, cols], ALU.mult, ALU.mult)
            g5 = work.tile([P, P3], F32, name="g5", bufs=1)
            for cols, entries in halves(P3):
                nc.vector.tensor_copy(g5[:, cols], a2[:].indirect(p5[:, entries]))
            for cols, entries in halves(P3):
                nc.vector.tensor_tensor(a3[:, t, cols], a2[:].indirect(p6[:, entries]), g5[:, cols], ALU.add)

        hs = [keep.tile([P, S], F32, name="h0")]
        hs = hs + [work.tile([P, S], F32, name=f"h{t}", bufs=1) for t in range(1, PACK)]
        ths = [work.tile([P, S], F32, name=f"th{t}", bufs=1, align_bytes=64) for t in range(PACK)]

        def finish(t, c):
            style_tanh(t, c, ths[t])
            cols = slice(c * CHUNK, (c + 1) * CHUNK)
            engine = nc.vector if c == CHUNKS - 1 else nc.gpsimd
            engine.tensor_tensor(hs[t][:, cols], hs[t][:, cols], ths[t][:, cols], ALU.add)

        w3_codes = keep.tile([P, N], U32, name="w3_codes", align_bytes=64)
        w3_scales = keep.tile([P, N], U8, name="w3_scales", align_bytes=64)

        def prepare_w3():
            raw = keep.tile([P, PACK, N], F32, name="w3_raw", tag="table1", align_bytes=64)
            nc.sync.dma_start(raw[:], w3.rearrange("(p j) c -> p j c", j=PACK))
            for g in range(2):
                rounded = ths[3][:].bitcast(BF16)[:, g * 512 * PACK : (g + 1) * 512 * PACK]
                nc.scalar.copy(
                    rounded.rearrange("p (t m j) -> p m t j", t=PACK, j=PACK),
                    raw[:, :, g * 512 : (g + 1) * 512].rearrange("p j (m t) -> p m t j", t=PACK),
                )
                cols = slice(g * 512, (g + 1) * 512)
                nc.vector.quantize_mx(out=w3_codes[:, cols].bitcast(E4M3), scales=w3_scales[:, cols], in_=rounded)

        sine_transposed(0, 0, hs[0], *phase_transposed(0, 0))
        w1_q = prepare_w1(0, 1, "turns")
        sine_direct(0, 1, hs[0])
        for c in range(CHUNKS):
            finish(0, c)
            if c + 2 < CHUNKS:
                sine_direct(0, c + 2, hs[0])
        w1_q.extend(prepare_w1(1, PACK - 1, "w1_bf"))
        levels(0, hs[0])

        steps = [(t, c) for t in range(1, PACK) for c in range(CHUNKS)]
        ahead = phase_transposed(*steps[0])
        for i, (t, c) in enumerate(steps):
            terms = ahead
            if i + 1 < len(steps):
                ahead = phase_transposed(*steps[i + 1])
            sine_transposed(t, c, hs[t], *terms)
            finish(t, c)
            if c == CHUNKS - 1:
                if t == PACK - 1:
                    prepare_w3()
                levels(t, hs[t])

        a3_bf = keep.tile([P, P3 * PACK], BF16, name="a3_bf", align_bytes=64)
        nc.vector.tensor_copy(a3_bf[:].rearrange("p (j t) -> p j t", t=PACK), a3[:].rearrange("p t j -> p j t"))
        a3_codes = keep.tile([P, P3], U32, name="a3_codes", align_bytes=64)
        a3_scales = keep.tile([P, P3], U8, name="a3_scales", align_bytes=64)
        nc.vector.quantize_mx(out=a3_codes[:].bitcast(E4M3), scales=a3_scales[:], in_=a3_bf[:])

        y_scales = keep.tile([P, 2, P3], U8, name="y_scales", align_bytes=64)
        ys = [keep.tile([P, PACK, P3], F32, name=f"y{g}") for g in range(2)]
        for g in range(2):
            for half in range(2):
                bank = banks[2 * g + half][:].rearrange("p (e j) -> p e j", e=2)
                for e in range(2):
                    cols = slice(g * 512 + (2 * half + e) * P, g * 512 + (2 * half + e + 1) * P)
                    nc.tensor.matmul_mx(
                        out=bank[:, e, :], lhsT=w3_codes[:, cols].bitcast(E4M3), lhsT_scale=w3_scales[:, cols],
                        rhs=a3_codes[:].bitcast(E4M3), rhs_scale=a3_scales[:], start=True, stop=True,
                    )
                copy = nc.scalar.copy if half == 0 else nc.vector.tensor_copy
                copy(ys[g][:, 2 * half : 2 * half + 2, :], bank)
            nc.sync.dma_start(out_0[g * 512 : (g + 1) * 512, :].rearrange("(p u) j -> p u j", u=PACK), ys[g][:])
        for g in range(2):
            y_bf = keep.tile([P, P3 * PACK], BF16, name=f"y_bf{g}", align_bytes=64)
            copy = nc.vector.tensor_copy if g == 0 else nc.scalar.copy
            copy(y_bf[:].rearrange("p (j u) -> p j u", u=PACK), ys[g][:].rearrange("p u j -> p j u"))
            y_codes = keep.tile([P, P3], U32, name=f"y_codes{g}", align_bytes=64)
            nc.vector.quantize_mx(out=y_codes[:].bitcast(E4M3), scales=y_scales[:, g, :], in_=y_bf[:])
            nc.sync.dma_start(out_1[g].rearrange("p m t -> p (m t)").bitcast(I32), y_codes[:].bitcast(I32))
        for q in range(4):
            nc.scalar.dma_start(
                out_2[:, 4 * q : 4 * q + 4, :].rearrange("g q m -> q g m").bitcast(I32),
                y_scales[32 * q : 32 * q + 4, :, :].bitcast(I32),
            )
